import numpy as np
import ml_dtypes


def mxq(x, axis, fmt="e4m3"):
    dtype, down = {"e4m3": (ml_dtypes.float8_e4m3fn, 7), "e5m2": (ml_dtypes.float8_e5m2, 14)}[fmt]
    v = np.moveaxis(np.asarray(x, np.float32).astype(ml_dtypes.bfloat16).astype(np.float64), axis, -1)
    blocks = v.reshape(v.shape[:-1] + (-1, 32))
    amax = np.abs(blocks).max(-1, keepdims=True)
    byte = np.maximum(np.where(amax > 0, np.frexp(amax)[1] - 1 + 127, 0) - down, 1)
    scale = np.exp2(byte - 127.0)
    codes = (blocks / scale).astype(np.float32).astype(dtype).astype(np.float64)
    return np.moveaxis((codes * scale).reshape(v.shape), -1, axis)


WIDE = False


def mx_kscale(k):
    if not WIDE:
        return np.ones(k)
    levels = np.array([10, -10, 5, -5, 0])
    if k % 512:
        return np.exp2(np.random.permutation(np.resize(levels, k // 32))).repeat(32)
    a = np.empty((k // 512, 16))
    for p in range(k // 512):
        a[p, :8] = np.random.permutation(np.resize(levels, 8))
        for g in range(8):
            far = levels[np.abs(levels - a[p, g]) >= 10]
            a[p, g + 8] = far[np.random.randint(len(far))]
    return np.exp2(a.ravel()).repeat(32)


def f64(x):
    return np.asarray(x).astype(np.float64)


def striped(idx):
    return np.tile(idx.reshape(-1, 16).T, (8, 1)).astype(np.uint16)


def unstriped(offs):
    return offs[:16].T.reshape(-1).astype(np.int64)


E2M1 = np.array([0.0, 0.5, 1.0, 1.5, 2.0, 3.0, 4.0, 6.0, -0.0, -0.5, -1.0, -1.5, -2.0, -3.0, -4.0, -6.0])


def pack_weight(w, fmt):
    k, n = w.shape
    w = f64(np.asarray(w, np.float32).astype(ml_dtypes.bfloat16)).reshape(k // 32, 32, n)
    amax = np.abs(w).max(1)
    if fmt == "e4m3":
        byte = np.frexp(amax)[1] - 1 + 127 - 7
    else:
        mant, ex = np.frexp(amax / 6.0)
        byte = np.where(mant > 0.5, ex, ex - 1) + 127
    byte = np.clip(np.where(amax > 0, byte, 1), 1, 254)
    scaled = (w * np.exp2(127.0 - byte)[:, None, :]).reshape(k, n).astype(np.float32)
    by_word = np.ascontiguousarray(scaled.reshape(k // 512, 128, 4, n).transpose(0, 1, 3, 2))
    if fmt == "e4m3":
        words = by_word.astype(ml_dtypes.float8_e4m3fn).view(np.uint8)
    else:
        c = by_word.astype(ml_dtypes.float4_e2m1fn).view(np.uint8) & 0xF
        words = (c[..., 0::2] | (c[..., 1::2] << 4)).reshape(k // 512, 128, 2 * n)
    return np.ascontiguousarray(words), np.ascontiguousarray(byte.astype(np.uint8).reshape(k // 512, 16, n))


def unpack_weight(words, scales, fmt):
    g, _, n = scales.shape
    words = np.ascontiguousarray(words).reshape(g, 128, n, -1)
    if fmt == "e4m3":
        vals = words.view(ml_dtypes.float8_e4m3fn).astype(np.float64)
    else:
        nib = np.empty((g, 128, n, 4), np.uint8)
        nib[..., 0::2] = words & 0xF
        nib[..., 1::2] = words >> 4
        vals = E2M1[nib]
    vals = vals * np.repeat(np.exp2(scales.astype(np.float64) - 127.0), 8, axis=1)[..., None]
    return vals.transpose(0, 1, 3, 2).reshape(g * 512, n)


def gelu(v):
    return 0.5 * v * (1.0 + np.tanh(np.sqrt(2.0 / np.pi) * (v + 0.044715 * v**3)))


K, T, H, S, S2, T3, P = 1536, 4096, 512, 1024, 1024, 2048, 512

def setup_inputs():
    n = np.random.standard_normal
    ks = mx_kscale(K)[:, None]
    u = mx_kscale(H)[:, None]
    d = {}
    d["tab_words"], d["tab_scales"] = pack_weight(n((K, T)) * ks, "e4m3")
    d["offs"] = striped(np.random.permutation(T)[:S])
    d["tab2_words"], d["tab2_scales"] = pack_weight(n((H, T3)) / u / H ** 0.5, "e4m3")
    d["offs2"] = striped(np.random.permutation(T3)[:S2])
    d["pos1"] = striped(np.random.permutation(S)[:P])
    d["pos2"] = striped(np.random.permutation(S)[:P])
    d["w1"] = (0.7 * n((K, H)) / ks * u.T / K ** 0.5).astype(np.float32)
    d["w4_words"], d["w4_scales"] = pack_weight(1.5 * n((K, H)) / ks / K ** 0.5, "e2m1")
    d["bias"] = (0.7 * n(H)).astype(np.float32)
    d["gain"] = (1.3 * np.exp(0.3 * n(H)) * u[:, 0]).astype(np.float32)
    d["song"] = n((S2, P)).astype(np.float32)
    return d

def reference(tab_words, tab_scales, offs, tab2_words, tab2_scales, offs2, pos1, pos2, w1, w4_words, w4_scales, bias, gain, song):
    v = unpack_weight(tab_words, tab_scales, "e4m3")[:, unstriped(offs)]
    v2 = unpack_weight(tab2_words, tab2_scales, "e4m3")[:, unstriped(offs2)]
    w4 = unpack_weight(w4_words, w4_scales, "e2m1")
    s = mxq(f64(w1), 0, "e4m3").T @ v
    b = w4.T @ v
    h = f64(gain)[:, None] * np.tanh(b + f64(bias)[:, None]) + s
    e = v2.T @ mxq(h, 0, "e4m3")
    verse = e[:, unstriped(pos1)]
    chorus = e[:, unstriped(pos2)]
    out = np.maximum(verse, chorus) * f64(song) - verse
    return out

@@ -1,0 +1,271 @@
+from contextlib import ExitStack
+
+import concourse.mybir as mybir
+
+K, T, H, S, S2, T3, NP = 1536, 4096, 512, 1024, 1024, 2048, 512
+FLOPS = 2 * (2 * K * H * S + H * S2 * S)
+
+F32 = mybir.dt.float32
+BF16 = mybir.dt.bfloat16
+I32 = mybir.dt.int32
+U32 = mybir.dt.uint32
+U16 = mybir.dt.uint16
+U8 = mybir.dt.uint8
+FP8X4 = mybir.dt.float8_e4m3fn_x4
+FP4X4 = mybir.dt.float4_e2m1fn_x4
+ALU = mybir.AluOpType
+ACT = mybir.ActivationFunctionType
+
+P = 128
+PASSES = K // 512
+BANK = 512
+HALVES = S // BANK
+M_TILES = S2 // P
+ROW0 = 32 - 4 * PASSES
+EARLY = 256
+W1_PIECES = [[(0, H)], [(0, H)], [(0, H // 2), (H // 2, H)]]
+
+
+def tile_list_karaoke_style_scores_kernel(
+    tc, tab_words, tab_scales, offs, tab2_words, tab2_scales, offs2, pos1, pos2, w1, w4_words, w4_scales, bias, gain, song, out
+):
+    nc = tc.nc
+    with ExitStack() as ctx:
+        keep = ctx.enter_context(tc.tile_pool(name="keep", bufs=1))
+        ring = ctx.enter_context(tc.tile_pool(name="ring", bufs=3))
+        psum = ctx.enter_context(tc.psum_pool(name="psum", bufs=1))
+
+        def bank_tile(index, name):
+            return psum.tile([P, BANK], F32, name=name, tag=f"bank{index}")
+
+        idx = keep.tile([P, S // 16], U16, name="idx")
+        idx2 = keep.tile([P, S2 // 16], U16, name="idx2")
+        p1 = keep.tile([P, NP // 16], U16, name="p1")
+        p2 = keep.tile([P, NP // 16], U16, name="p2")
+        tab_w = [keep.tile([P, T], I32, name=f"tab_w{a}", align_bytes=64) for a in range(PASSES)]
+        tab_s = keep.tile([P, T], U8, name="tab_s", align_bytes=64)
+        tab2_w = keep.tile([P, T3], I32, name="tab2_w", align_bytes=64)
+        tab2_s = keep.tile([P, T3], U8, name="tab2_s", align_bytes=64)
+        w4_raw = keep.tile([P, PASSES, 2 * H], U8, name="w4_raw", align_bytes=64)
+        w4_s_raw = keep.tile([P, PASSES, H], U8, name="w4_s_raw", align_bytes=64)
+        w1_raw = [
+            [keep.tile([P, 4, c1 - c0], F32, name=f"w1_raw{a}_{c0}") for c0, c1 in W1_PIECES[a]] for a in range(PASSES)
+        ]
+        bias_t = keep.tile([P, 4], F32, name="bias_t")
+        gain_t = keep.tile([P, 4], F32, name="gain_t")
+        song_t = [keep.tile([P, M_TILES // 2, NP], F32, name=f"song_t{g}") for g in range(2)]
+        v_s_shift = [keep.tile([P, S], U8, name=f"v_s_shift{a}", align_bytes=64) for a in range(PASSES)]
+
+        for q in range(4):
+            nc.vector.memset(tab_s[32 * q : 32 * q + ROW0, :].bitcast(I32), 0)
+        nc.gpsimd.memset(w4_s_raw[:].rearrange("p a c -> p (a c)").bitcast(I32), 0)
+        nc.gpsimd.memset(tab2_s[:].bitcast(I32), 0)
+        for plane in v_s_shift:
+            nc.gpsimd.memset(plane[:].bitcast(I32), 0)
+
+        def load_tab(a):
+            nc.sync.dma_start(out=tab_w[a][:], in_=tab_words[a].rearrange("p t i -> p (t i)").bitcast(I32))
+
+        def load_w1(a, piece):
+            c0, c1 = W1_PIECES[a][piece]
+            rows = w1[512 * a : 512 * (a + 1), c0:c1]
+            nc.sync.dma_start(out=w1_raw[a][piece][:], in_=rows.rearrange("(p j) c -> p j c", j=4))
+
+        nc.sync.dma_start(idx[:], offs)
+        for q in range(4):
+            nc.sync.dma_start(
+                out=tab_s[32 * q + ROW0 : 32 * (q + 1), :].bitcast(I32),
+                in_=tab_scales[:, 4 * q : 4 * q + 4, :].bitcast(I32),
+            )
+        nc.sync.dma_start(out=w4_raw[:].bitcast(I32), in_=w4_words.rearrange("a p c -> p a c").bitcast(I32))
+        load_tab(0)
+        nc.sync.dma_start(idx2[:], offs2)
+        for q in range(4):
+            nc.sync.dma_start(
+                out=w4_s_raw[32 * q : 32 * q + 4, :, :].bitcast(I32),
+                in_=w4_scales[:, 4 * q : 4 * q + 4, :].rearrange("a r c -> r a c").bitcast(I32),
+            )
+        load_tab(1)
+        nc.sync.dma_start(out=bias_t[:], in_=bias.rearrange("(p t) -> p t", t=4))
+        for q in range(4):
+            nc.gpsimd.dma_start(
+                out=tab2_s[32 * q : 32 * q + 4, :].bitcast(I32),
+                in_=tab2_scales[0, 4 * q : 4 * q + 4, :].bitcast(I32),
+            )
+
+        v_s = keep.tile([P, S], U8, name="v_s", align_bytes=64)
+        nc.vector.tensor_copy(v_s[:], tab_s[:].indirect(idx[:]))
+        for a in range(PASSES):
+            first = ROW0 + 4 * a
+            nc.scalar.dma_start(
+                out=v_s_shift[a][0:100, :].bitcast(I32), in_=v_s[first : first + 100, :].bitcast(I32)
+            )
+        v_planes = v_s_shift
+
+        load_tab(2)
+        nc.sync.dma_start(out=gain_t[:], in_=gain.rearrange("(p t) -> p t", t=4))
+        load_w1(0, 0)
+        load_w1(1, 0)
+        load_w1(2, 0)
+        load_w1(2, 1)
+        nc.sync.dma_start(out=tab2_w[:], in_=tab2_words[0].rearrange("p t i -> p (t i)").bitcast(I32))
+        nc.sync.dma_start(p1[:], pos1)
+        nc.sync.dma_start(p2[:], pos2)
+        for g in range(2):
+            rows = song[g * S2 // 2 : (g + 1) * S2 // 2, :]
+            nc.sync.dma_start(out=song_t[g][:], in_=rows.rearrange("(c p) n -> p c n", p=P))
+
+        w4_w = keep.tile([P, PASSES, 2 * H], U8, name="w4_w", align_bytes=64)
+        w4_s = keep.tile([P, PASSES, H], U8, name="w4_s", align_bytes=64)
+        nc.vector.tensor_copy(
+            out=w4_w[:].bitcast(U16).rearrange("p a (t m) -> p t a m", t=4),
+            in_=w4_raw[:].bitcast(U16).rearrange("p a (m t) -> p t a m", t=4),
+        )
+        nc.vector.tensor_copy(
+            out=w4_s[:].rearrange("p a (t m) -> p t a m", t=4),
+            in_=w4_s_raw[:].rearrange("p a (m t) -> p t a m", t=4),
+        )
+
+        v_w = [[keep.tile([P, BANK], U32, name=f"v_w{a}_{u}", align_bytes=64) for u in range(HALVES)] for a in range(PASSES)]
+        w1_bf = [keep.tile([P, 4 * H], BF16, name=f"w1_bf{a}", align_bytes=64) for a in range(PASSES)]
+        w1_w = [keep.tile([P, H], U32, name=f"w1_w{a}", align_bytes=64) for a in range(PASSES)]
+        w1_s = [keep.tile([P, H], U8, name=f"w1_s{a}", align_bytes=64) for a in range(PASSES)]
+
+        def gather_tab(a):
+            for u in range(HALVES):
+                nc.vector.tensor_copy(v_w[a][u][:], tab_w[a][:].bitcast(U32).indirect(idx[:, 32 * u : 32 * (u + 1)]))
+
+        def round_w1(copy, a, piece):
+            c0, c1 = W1_PIECES[a][piece]
+            copy(
+                out=w1_bf[a][:].rearrange("p (t m j) -> p m j t", t=4, j=4)[:, c0 // 4 : c1 // 4],
+                in_=w1_raw[a][piece][:].rearrange("p j (m t) -> p m j t", t=4),
+            )
+
+        def quantise_w1(a):
+            nc.vector.quantize_mx(out=w1_w[a][:].bitcast(FP8X4), scales=w1_s[a][:], in_=w1_bf[a][:])
+
+        b_acc = [[bank_tile(4 * u + t, f"b_acc{u}_{t}") for t in range(4)] for u in range(HALVES)]
+
+        def b_pass(a):
+            for u in range(HALVES):
+                for t in range(4):
+                    nc.tensor.matmul_mx(
+                        out=b_acc[u][t][:],
+                        lhsT=w4_w[:, a, 2 * P * t : 2 * P * (t + 1)].bitcast(FP4X4),
+                        lhsT_scale=w4_s[:, a, P * t : P * (t + 1)],
+                        rhs=v_w[a][u][:].bitcast(FP8X4),
+                        rhs_scale=v_planes[a][:, BANK * u : BANK * (u + 1)],
+                        start=(a == 0),
+                        stop=(a == PASSES - 1),
+                    )
+
+        v2_s = keep.tile([P, S2], U8, name="v2_s", align_bytes=64)
+
+        gather_tab(0)
+        b_pass(0)
+        gather_tab(1)
+        nc.vector.tensor_copy(v2_s[:], tab2_s[:].indirect(idx2[:]))
+        b_pass(1)
+        gather_tab(2)
+        b_pass(2)
+
+        th = [[keep.tile([P, BANK], F32, name=f"th{u}_{t}") for t in range(4)] for u in range(HALVES)]
+        for u in range(HALVES):
+            for t in range(4):
+                nc.scalar.activation(out=th[u][t][:], in_=b_acc[u][t][:], func=ACT.Tanh, bias=bias_t[:, t : t + 1])
+
+        for a in range(PASSES):
+            for piece in range(len(W1_PIECES[a])):
+                round_w1(nc.scalar.copy if (a, piece) == (2, 0) else nc.vector.tensor_copy, a, piece)
+            quantise_w1(a)
+
+        s_acc = [[bank_tile(4 * u + t, f"s_acc{u}_{t}") for t in range(4)] for u in range(HALVES)]
+
+        def s_pass(a, u, t):
+            nc.tensor.matmul_mx(
+                out=s_acc[u][t][:],
+                lhsT=w1_w[a][:, P * t : P * (t + 1)].bitcast(FP8X4),
+                lhsT_scale=w1_s[a][:, P * t : P * (t + 1)],
+                rhs=v_w[a][u][:].bitcast(FP8X4),
+                rhs_scale=v_planes[a][:, BANK * u : BANK * (u + 1)],
+                start=(a == 0),
+                stop=(a == PASSES - 1),
+            )
+
+        for a in range(PASSES):
+            for u in range(HALVES):
+                for t in range(4):
+                    s_pass(a, u, t)
+
+        h_rows = [keep.tile([P, 4, BANK], BF16, name=f"h_rows{u}", tag=f"h_rows{u}", align_bytes=64) for u in range(HALVES)]
+        h_bf = [keep.tile([P, BANK, 4], BF16, name=f"h_bf{u}", align_bytes=64) for u in range(HALVES)]
+        h_w = [keep.tile([P, BANK], U32, name=f"h_w{u}", align_bytes=64) for u in range(HALVES)]
+        h_s = [keep.tile([P, BANK], U8, name=f"h_s{u}", align_bytes=64) for u in range(HALVES)]
+
+        def weave(copy, u, c0, c1):
+            copy(
+                out=h_bf[u][:, c0:c1, :].rearrange("p (c i) t -> p c t i", i=4),
+                in_=h_rows[u][:, :, c0:c1].rearrange("p t (c i) -> p c t i", i=4),
+            )
+
+        for u in range(HALVES):
+            for t in range(4):
+                nc.vector.scalar_tensor_tensor(
+                    out=h_rows[u][:, t, :], in0=th[u][t][:], scalar=gain_t[:, t : t + 1], in1=s_acc[u][t][:],
+                    op0=ALU.mult, op1=ALU.add,
+                )
+        v2_early = keep.tile([P, EARLY], U32, name="v2_early", align_bytes=64)
+        nc.vector.tensor_copy(v2_early[:], tab2_w[:].bitcast(U32).indirect(idx2[:, 0 : EARLY // 16]))
+        weave(nc.scalar.copy, 0, 0, BANK)
+        weave(nc.vector.tensor_copy, 1, 0, 384)
+        weave(nc.scalar.copy, 1, 384, BANK)
+        for u in range(HALVES):
+            nc.vector.quantize_mx(
+                out=h_w[u][:].bitcast(FP8X4), scales=h_s[u][:], in_=h_bf[u][:].rearrange("p c t -> p (c t)")
+            )
+        v2_late = keep.tile([P, S2 - EARLY], U32, name="v2_late", tag="h_rows1", align_bytes=64)
+        nc.vector.tensor_copy(v2_late[:], tab2_w[:].bitcast(U32).indirect(idx2[:, EARLY // 16 :]))
+
+        def v2_words(i):
+            if P * i < EARLY:
+                return v2_early[:, P * i : P * (i + 1)]
+            return v2_late[:, P * i - EARLY : P * (i + 1) - EARLY]
+
+        for i in range(M_TILES):
+            e = ring.tile([P, S], F32, name="e")
+            for u in range(HALVES):
+                e_acc = bank_tile((HALVES * i + u) % 8, f"e_acc{i}_{u}")
+                nc.tensor.matmul_mx(
+                    out=e_acc[:],
+                    lhsT=v2_words(i).bitcast(FP8X4),
+                    lhsT_scale=v2_s[:, P * i : P * (i + 1)],
+                    rhs=h_w[u][:].bitcast(FP8X4),
+                    rhs_scale=h_s[u][:],
+                    start=True,
+                    stop=True,
+                )
+                nc.scalar.copy(out=e[:, BANK * u : BANK * (u + 1)], in_=e_acc[:])
+            verse = ring.tile([P, NP], F32, name="verse")
+            chorus = ring.tile([P, NP], F32, name="chorus")
+            best = ring.tile([P, NP], F32, name="best")
+            weighted = ring.tile([P, NP], F32, name="weighted")
+            result = ring.tile([P, NP], F32, name="result")
+            nc.vector.tensor_copy(verse[:], e[:].indirect(p1[:]))
+            for g in range(2):
+                nc.vector.tensor_copy(chorus[:, 256 * g : 256 * (g + 1)], e[:].indirect(p2[:, 16 * g : 16 * (g + 1)]))
+            for g in range(2):
+                cols = slice(256 * g, 256 * (g + 1))
+                nc.vector.tensor_tensor(out=best[:, cols], in0=verse[:, cols], in1=chorus[:, cols], op=ALU.max)
+            song_i = song_t[i // 4][:, i % 4, :]
+            if i < M_TILES - 1:
+                nc.gpsimd.tensor_tensor(out=weighted[:], in0=best[:], in1=song_i, op=ALU.mult)
+                nc.gpsimd.tensor_tensor(out=result[:], in0=weighted[:], in1=verse[:], op=ALU.subtract)
+            else:
+                for g in range(2):
+                    cols = slice(256 * g, 256 * (g + 1))
+                    nc.vector.tensor_tensor(out=weighted[:, cols], in0=best[:, cols], in1=song_i[:, cols], op=ALU.mult)
+                for g in range(2):
+                    cols = slice(256 * g, 256 * (g + 1))
+                    nc.vector.tensor_tensor(out=result[:, cols], in0=weighted[:, cols], in1=verse[:, cols], op=ALU.subtract)
+            nc.sync.dma_start(out=out[P * i : P * (i + 1), :], in_=result[:])

@@ -1,6 +1,7 @@
 from contextlib import ExitStack
 
 import concourse.mybir as mybir
+from concourse.masks import make_identity
 
 K, T, H, S, S2, T3, NP = 1536, 4096, 512, 1024, 1024, 2048, 512
 FLOPS = 2 * (2 * K * H * S + H * S2 * S)
@@ -21,7 +22,7 @@ PASSES = K // 512
 BANK = 512
 HALVES = S // BANK
 M_TILES = S2 // P
-ROW0 = 32 - 4 * PASSES
+TAB_S_FIRST = (48, 64, 80)
 EARLY = 256
 W1_PIECES = [[(0, H)], [(0, H)], [(0, H // 2), (H // 2, H)]]
 
@@ -32,7 +33,7 @@ def tile_list_karaoke_style_scores_kernel(
     nc = tc.nc
     with ExitStack() as ctx:
         keep = ctx.enter_context(tc.tile_pool(name="keep", bufs=1))
-        ring = ctx.enter_context(tc.tile_pool(name="ring", bufs=3))
+        ring = ctx.enter_context(tc.tile_pool(name="ring", bufs=4))
         psum = ctx.enter_context(tc.psum_pool(name="psum", bufs=1))
 
         def bank_tile(index, name):
@@ -45,23 +46,27 @@ def tile_list_karaoke_style_scores_kernel(
         tab_w = [keep.tile([P, T], I32, name=f"tab_w{a}", align_bytes=64) for a in range(PASSES)]
         tab_s = keep.tile([P, T], U8, name="tab_s", align_bytes=64)
         tab2_w = keep.tile([P, T3], I32, name="tab2_w", align_bytes=64)
-        tab2_s = keep.tile([P, T3], U8, name="tab2_s", align_bytes=64)
+        tab2_s = keep.tile([P, T3], U8, name="tab2_s", tag="v_w2_0", align_bytes=64)
         w4_raw = keep.tile([P, PASSES, 2 * H], U8, name="w4_raw", align_bytes=64)
-        w4_s_raw = keep.tile([P, PASSES, H], U8, name="w4_s_raw", align_bytes=64)
+        w4_s_raw = keep.tile([P, PASSES, H], U8, name="w4_s_raw", tag="v_w1_0", align_bytes=64)
         w1_raw = [
             [keep.tile([P, 4, c1 - c0], F32, name=f"w1_raw{a}_{c0}") for c0, c1 in W1_PIECES[a]] for a in range(PASSES)
         ]
         bias_t = keep.tile([P, 4], F32, name="bias_t")
         gain_t = keep.tile([P, 4], F32, name="gain_t")
         song_t = [keep.tile([P, M_TILES // 2, NP], F32, name=f"song_t{g}") for g in range(2)]
-        v_s_shift = [keep.tile([P, S], U8, name=f"v_s_shift{a}", align_bytes=64) for a in range(PASSES)]
+        v_planes = keep.tile([P, PASSES, S], U8, name="v_planes", align_bytes=64)
+        ident = keep.tile([P, P], F32, name="ident")
 
-        for q in range(4):
-            nc.vector.memset(tab_s[32 * q : 32 * q + ROW0, :].bitcast(I32), 0)
-        nc.gpsimd.memset(w4_s_raw[:].rearrange("p a c -> p (a c)").bitcast(I32), 0)
-        nc.gpsimd.memset(tab2_s[:].bitcast(I32), 0)
-        for plane in v_s_shift:
-            nc.gpsimd.memset(plane[:].bitcast(I32), 0)
+        v2_s = keep.tile([P, S2], U8, name="v2_s", align_bytes=64)
+
+        nc.vector.memset(w4_s_raw[:].rearrange("p a c -> p (a c)").bitcast(I32), 0)
+        nc.vector.memset(tab_s[0:48, :].bitcast(I32), 0)
+        nc.gpsimd.memset(tab_s[96:P, :].bitcast(I32), 0)
+        nc.gpsimd.memset(tab2_s[0:112, :].bitcast(I32), 0)
+        nc.gpsimd.memset(v_planes[:].rearrange("p a c -> p (a c)").bitcast(I32), 0)
+        nc.gpsimd.memset(v2_s[:].bitcast(I32), 0)
+        make_identity(nc, ident[:])
 
         def load_tab(a):
             nc.sync.dma_start(out=tab_w[a][:], in_=tab_words[a].rearrange("p t i -> p (t i)").bitcast(I32))
@@ -71,45 +76,48 @@ def tile_list_karaoke_style_scores_kernel(
             rows = w1[512 * a : 512 * (a + 1), c0:c1]
             nc.sync.dma_start(out=w1_raw[a][piece][:], in_=rows.rearrange("(p j) c -> p j c", j=4))
 
-        nc.sync.dma_start(idx[:], offs)
-        for q in range(4):
+        def place_rows(plane, gathered, first, q):
             nc.sync.dma_start(
-                out=tab_s[32 * q + ROW0 : 32 * (q + 1), :].bitcast(I32),
-                in_=tab_scales[:, 4 * q : 4 * q + 4, :].bitcast(I32),
+                out=plane[32 * q : 32 * q + 4, :].bitcast(I32),
+                in_=gathered[first + 4 * q : first + 4 * q + 4, :].bitcast(I32),
             )
-        nc.sync.dma_start(out=w4_raw[:].bitcast(I32), in_=w4_words.rearrange("a p c -> p a c").bitcast(I32))
-        load_tab(0)
+
+        scale_rows = tab_scales.rearrange("a q t -> (a q) t").bitcast(I32)
+        nc.sync.dma_start(idx[:], offs)
+        nc.sync.dma_start(out=tab_s[48:64, :].bitcast(I32), in_=scale_rows[0:16, :])
+        nc.sync.dma_start(out=tab_s[64:96, :].bitcast(I32), in_=scale_rows[16:48, :])
         nc.sync.dma_start(idx2[:], offs2)
+        nc.sync.dma_start(out=tab2_s[112:P, :].bitcast(I32), in_=tab2_scales[0].bitcast(I32))
+        nc.sync.dma_start(out=w4_raw[:].bitcast(I32), in_=w4_words.rearrange("a p c -> p a c").bitcast(I32))
+        nc.sync.dma_start(out=bias_t[:], in_=bias.rearrange("(p t) -> p t", t=4))
+        load_tab(0)
         for q in range(4):
             nc.sync.dma_start(
                 out=w4_s_raw[32 * q : 32 * q + 4, :, :].bitcast(I32),
                 in_=w4_scales[:, 4 * q : 4 * q + 4, :].rearrange("a r c -> r a c").bitcast(I32),
             )
+        nc.sync.dma_start(out=gain_t[:], in_=gain.rearrange("(p t) -> p t", t=4))
+        nc.sync.dma_start(p1[:], pos1)
         load_tab(1)
-        nc.sync.dma_start(out=bias_t[:], in_=bias.rearrange("(p t) -> p t", t=4))
-        for q in range(4):
-            nc.gpsimd.dma_start(
-                out=tab2_s[32 * q : 32 * q + 4, :].bitcast(I32),
-                in_=tab2_scales[0, 4 * q : 4 * q + 4, :].bitcast(I32),
-            )
 
         v_s = keep.tile([P, S], U8, name="v_s", align_bytes=64)
         nc.vector.tensor_copy(v_s[:], tab_s[:].indirect(idx[:]))
-        for a in range(PASSES):
-            first = ROW0 + 4 * a
-            nc.scalar.dma_start(
-                out=v_s_shift[a][0:100, :].bitcast(I32), in_=v_s[first : first + 100, :].bitcast(I32)
-            )
-        v_planes = v_s_shift
+        v2_s_rows = keep.tile([P, S2], U8, name="v2_s_rows", align_bytes=64)
+        nc.vector.tensor_copy(v2_s_rows[:], tab2_s[:].indirect(idx2[:]))
 
+        moves = [(a, q) for a in range(PASSES) for q in range(4)]
+        for a, q in moves[:6]:
+            place_rows(v_planes[:, a, :], v_s, TAB_S_FIRST[a], q)
         load_tab(2)
-        nc.sync.dma_start(out=gain_t[:], in_=gain.rearrange("(p t) -> p t", t=4))
+        for a, q in moves[6:]:
+            place_rows(v_planes[:, a, :], v_s, TAB_S_FIRST[a], q)
         load_w1(0, 0)
         load_w1(1, 0)
         load_w1(2, 0)
         load_w1(2, 1)
         nc.sync.dma_start(out=tab2_w[:], in_=tab2_words[0].rearrange("p t i -> p (t i)").bitcast(I32))
-        nc.sync.dma_start(p1[:], pos1)
+        for q in range(4):
+            place_rows(v2_s[:], v2_s_rows, 112, q)
         nc.sync.dma_start(p2[:], pos2)
         for g in range(2):
             rows = song[g * S2 // 2 : (g + 1) * S2 // 2, :]
@@ -126,13 +134,14 @@ def tile_list_karaoke_style_scores_kernel(
             in_=w4_s_raw[:].rearrange("p a (m t) -> p t a m", t=4),
         )
 
-        v_w = [[keep.tile([P, BANK], U32, name=f"v_w{a}_{u}", align_bytes=64) for u in range(HALVES)] for a in range(PASSES)]
+        v_w = [[] for a in range(PASSES)]
         w1_bf = [keep.tile([P, 4 * H], BF16, name=f"w1_bf{a}", align_bytes=64) for a in range(PASSES)]
         w1_w = [keep.tile([P, H], U32, name=f"w1_w{a}", align_bytes=64) for a in range(PASSES)]
         w1_s = [keep.tile([P, H], U8, name=f"w1_s{a}", align_bytes=64) for a in range(PASSES)]
 
         def gather_tab(a):
             for u in range(HALVES):
+                v_w[a].append(keep.tile([P, BANK], U32, name=f"v_w{a}_{u}", tag=f"v_w{a}_{u}", align_bytes=64))
                 nc.vector.tensor_copy(v_w[a][u][:], tab_w[a][:].bitcast(U32).indirect(idx[:, 32 * u : 32 * (u + 1)]))
 
         def round_w1(copy, a, piece):
@@ -155,17 +164,14 @@ def tile_list_karaoke_style_scores_kernel(
                         lhsT=w4_w[:, a, 2 * P * t : 2 * P * (t + 1)].bitcast(FP4X4),
                         lhsT_scale=w4_s[:, a, P * t : P * (t + 1)],
                         rhs=v_w[a][u][:].bitcast(FP8X4),
-                        rhs_scale=v_planes[a][:, BANK * u : BANK * (u + 1)],
+                        rhs_scale=v_planes[:, a, BANK * u : BANK * (u + 1)],
                         start=(a == 0),
                         stop=(a == PASSES - 1),
                     )
 
-        v2_s = keep.tile([P, S2], U8, name="v2_s", align_bytes=64)
-
         gather_tab(0)
         b_pass(0)
         gather_tab(1)
-        nc.vector.tensor_copy(v2_s[:], tab2_s[:].indirect(idx2[:]))
         b_pass(1)
         gather_tab(2)
         b_pass(2)
@@ -188,7 +194,7 @@ def tile_list_karaoke_style_scores_kernel(
                 lhsT=w1_w[a][:, P * t : P * (t + 1)].bitcast(FP8X4),
                 lhsT_scale=w1_s[a][:, P * t : P * (t + 1)],
                 rhs=v_w[a][u][:].bitcast(FP8X4),
-                rhs_scale=v_planes[a][:, BANK * u : BANK * (u + 1)],
+                rhs_scale=v_planes[:, a, BANK * u : BANK * (u + 1)],
                 start=(a == 0),
                 stop=(a == PASSES - 1),
             )
@@ -232,10 +238,12 @@ def tile_list_karaoke_style_scores_kernel(
                 return v2_early[:, P * i : P * (i + 1)]
             return v2_late[:, P * i - EARLY : P * (i + 1) - EARLY]
 
-        for i in range(M_TILES):
-            e = ring.tile([P, S], F32, name="e")
+        e, verse, chorus = {}, {}, {}
+
+        def scores(i):
+            e[i] = ring.tile([P, S], F32, name="e")
             for u in range(HALVES):
-                e_acc = bank_tile((HALVES * i + u) % 8, f"e_acc{i}_{u}")
+                e_acc = bank_tile((HALVES * i + u) % 4, f"e_acc{i}_{u}")
                 nc.tensor.matmul_mx(
                     out=e_acc[:],
                     lhsT=v2_words(i).bitcast(FP8X4),
@@ -245,27 +253,67 @@ def tile_list_karaoke_style_scores_kernel(
                     start=True,
                     stop=True,
                 )
-                nc.scalar.copy(out=e[:, BANK * u : BANK * (u + 1)], in_=e_acc[:])
-            verse = ring.tile([P, NP], F32, name="verse")
-            chorus = ring.tile([P, NP], F32, name="chorus")
-            best = ring.tile([P, NP], F32, name="best")
-            weighted = ring.tile([P, NP], F32, name="weighted")
+                nc.scalar.copy(out=e[i][:, BANK * u : BANK * (u + 1)], in_=e_acc[:])
+
+        def pick(i):
+            verse[i] = ring.tile([P, NP], F32, name="verse")
+            chorus[i] = ring.tile([P, NP], F32, name="chorus")
+            nc.vector.tensor_copy(verse[i][:], e[i][:].indirect(p1[:]))
+            nc.vector.tensor_copy(chorus[i][:], e[i][:].indirect(p2[:]))
+
+        def song_rows(i):
+            return song_t[i // 4][:, i % 4, :]
+
+        def larger(i, cols):
+            nc.vector.tensor_tensor(out=chorus[i][:, cols], in0=chorus[i][:, cols], in1=verse[i][:, cols], op=ALU.max)
+
+        def weigh_negated(i):
+            nc.vector.scalar_tensor_tensor(
+                out=chorus[i][:], in0=chorus[i][:], scalar=-1.0, in1=song_rows(i), op0=ALU.mult, op1=ALU.mult
+            )
+
+        def finish_on_tensor(i):
+            turned = bank_tile(4 + i % 2, f"turned{i}")
+            for k, term in enumerate((verse[i], chorus[i])):
+                for c in range(4):
+                    nc.tensor.matmul(
+                        turned[:, P * c : P * (c + 1)], lhsT=term[:, P * c : P * (c + 1)], rhs=ident[:],
+                        is_transpose=True, start=(k == 0 and c == 0), stop=(k == 1 and c == 3),
+                    )
+            turned_sb = ring.tile([P, NP], F32, name="turned_sb")
+            nc.scalar.copy(out=turned_sb[:], in_=turned[:])
+            upright = bank_tile(6 + i % 2, f"upright{i}")
+            for c in range(4):
+                nc.tensor.transpose(upright[:, P * c : P * (c + 1)], turned_sb[:, P * c : P * (c + 1)], ident[:])
             result = ring.tile([P, NP], F32, name="result")
-            nc.vector.tensor_copy(verse[:], e[:].indirect(p1[:]))
-            for g in range(2):
-                nc.vector.tensor_copy(chorus[:, 256 * g : 256 * (g + 1)], e[:].indirect(p2[:, 16 * g : 16 * (g + 1)]))
-            for g in range(2):
-                cols = slice(256 * g, 256 * (g + 1))
-                nc.vector.tensor_tensor(out=best[:, cols], in0=verse[:, cols], in1=chorus[:, cols], op=ALU.max)
-            song_i = song_t[i // 4][:, i % 4, :]
-            if i < M_TILES - 1:
-                nc.gpsimd.tensor_tensor(out=weighted[:], in0=best[:], in1=song_i, op=ALU.mult)
-                nc.gpsimd.tensor_tensor(out=result[:], in0=weighted[:], in1=verse[:], op=ALU.subtract)
-            else:
-                for g in range(2):
-                    cols = slice(256 * g, 256 * (g + 1))
-                    nc.vector.tensor_tensor(out=weighted[:, cols], in0=best[:, cols], in1=song_i[:, cols], op=ALU.mult)
-                for g in range(2):
-                    cols = slice(256 * g, 256 * (g + 1))
-                    nc.vector.tensor_tensor(out=result[:, cols], in0=weighted[:, cols], in1=verse[:, cols], op=ALU.subtract)
+            nc.scalar.activation(out=result[:], in_=upright[:], func=ACT.Copy, scale=-1.0)
             nc.sync.dma_start(out=out[P * i : P * (i + 1), :], in_=result[:])
+
+        last = M_TILES - 1
+        scores(0)
+        scores(1)
+        for i in range(last):
+            if i + 2 <= last:
+                scores(i + 2)
+            pick(i)
+            if i > 0:
+                weigh_negated(i - 1)
+            larger(i, slice(0, NP))
+            if i > 0:
+                finish_on_tensor(i - 1)
+        pick(last)
+        weigh_negated(last - 1)
+        finish_on_tensor(last - 1)
+        col_halves = [slice(0, NP // 2), slice(NP // 2, NP)]
+        result = ring.tile([P, NP], F32, name="result")
+        for cols in col_halves:
+            larger(last, cols)
+        for cols in col_halves:
+            nc.vector.tensor_tensor(
+                out=chorus[last][:, cols], in0=chorus[last][:, cols], in1=song_rows(last)[:, cols], op=ALU.mult
+            )
+        for cols in col_halves:
+            nc.vector.tensor_tensor(
+                out=result[:, cols], in0=chorus[last][:, cols], in1=verse[last][:, cols], op=ALU.subtract
+            )
+        nc.sync.dma_start(out=out[P * last : P * (last + 1), :], in_=result[:])

@@ -239,6 +239,7 @@ def tile_list_karaoke_style_scores_kernel(
             return v2_late[:, P * i - EARLY : P * (i + 1) - EARLY]
 
         e, verse, chorus = {}, {}, {}
+        col_halves = [slice(0, NP // 2), slice(NP // 2, NP)]
 
         def scores(i):
             e[i] = ring.tile([P, S], F32, name="e")
@@ -259,7 +260,8 @@ def tile_list_karaoke_style_scores_kernel(
             verse[i] = ring.tile([P, NP], F32, name="verse")
             chorus[i] = ring.tile([P, NP], F32, name="chorus")
             nc.vector.tensor_copy(verse[i][:], e[i][:].indirect(p1[:]))
-            nc.vector.tensor_copy(chorus[i][:], e[i][:].indirect(p2[:]))
+            for g, cols in enumerate(col_halves):
+                nc.vector.tensor_copy(chorus[i][:, cols], e[i][:].indirect(p2[:, 16 * g : 16 * (g + 1)]))
 
         def song_rows(i):
             return song_t[i // 4][:, i % 4, :]
@@ -267,14 +269,15 @@ def tile_list_karaoke_style_scores_kernel(
         def larger(i, cols):
             nc.vector.tensor_tensor(out=chorus[i][:, cols], in0=chorus[i][:, cols], in1=verse[i][:, cols], op=ALU.max)
 
-        def weigh_negated(i):
-            nc.vector.scalar_tensor_tensor(
-                out=chorus[i][:], in0=chorus[i][:], scalar=-1.0, in1=song_rows(i), op0=ALU.mult, op1=ALU.mult
+        def weigh_on_gpsimd(i):
+            nc.gpsimd.tensor_tensor(out=chorus[i][:], in0=chorus[i][:], in1=song_rows(i), op=ALU.mult)
+            nc.gpsimd.tensor_scalar(
+                out=verse[i][:], in0=verse[i][:], scalar1=-1.0, scalar2=0.0, op0=ALU.mult, op1=ALU.add
             )
 
         def finish_on_tensor(i):
             turned = bank_tile(4 + i % 2, f"turned{i}")
-            for k, term in enumerate((verse[i], chorus[i])):
+            for k, term in enumerate((chorus[i], verse[i])):
                 for c in range(4):
                     nc.tensor.matmul(
                         turned[:, P * c : P * (c + 1)], lhsT=term[:, P * c : P * (c + 1)], rhs=ident[:],
@@ -286,34 +289,39 @@ def tile_list_karaoke_style_scores_kernel(
             for c in range(4):
                 nc.tensor.transpose(upright[:, P * c : P * (c + 1)], turned_sb[:, P * c : P * (c + 1)], ident[:])
             result = ring.tile([P, NP], F32, name="result")
-            nc.scalar.activation(out=result[:], in_=upright[:], func=ACT.Copy, scale=-1.0)
+            nc.scalar.copy(out=result[:], in_=upright[:])
             nc.sync.dma_start(out=out[P * i : P * (i + 1), :], in_=result[:])
 
-        last = M_TILES - 1
+        def finish_on_gpsimd(i):
+            result = ring.tile([P, NP], F32, name="result")
+            nc.gpsimd.tensor_tensor(out=chorus[i][:], in0=chorus[i][:], in1=song_rows(i), op=ALU.mult)
+            nc.gpsimd.tensor_tensor(out=result[:], in0=chorus[i][:], in1=verse[i][:], op=ALU.subtract)
+            nc.sync.dma_start(out=out[P * i : P * (i + 1), :], in_=result[:])
+
+        def finish_on_vector(i):
+            result = ring.tile([P, NP], F32, name="result")
+            for cols in col_halves:
+                nc.vector.tensor_tensor(
+                    out=chorus[i][:, cols], in0=chorus[i][:, cols], in1=song_rows(i)[:, cols], op=ALU.mult
+                )
+            for cols in col_halves:
+                nc.vector.tensor_tensor(
+                    out=result[:, cols], in0=chorus[i][:, cols], in1=verse[i][:, cols], op=ALU.subtract
+                )
+            nc.sync.dma_start(out=out[P * i : P * (i + 1), :], in_=result[:])
+
         scores(0)
         scores(1)
-        for i in range(last):
-            if i + 2 <= last:
+        for i in range(M_TILES):
+            if i + 2 < M_TILES:
                 scores(i + 2)
             pick(i)
-            if i > 0:
-                weigh_negated(i - 1)
-            larger(i, slice(0, NP))
-            if i > 0:
-                finish_on_tensor(i - 1)
-        pick(last)
-        weigh_negated(last - 1)
-        finish_on_tensor(last - 1)
-        col_halves = [slice(0, NP // 2), slice(NP // 2, NP)]
-        result = ring.tile([P, NP], F32, name="result")
-        for cols in col_halves:
-            larger(last, cols)
-        for cols in col_halves:
-            nc.vector.tensor_tensor(
-                out=chorus[last][:, cols], in0=chorus[last][:, cols], in1=song_rows(last)[:, cols], op=ALU.mult
-            )
-        for cols in col_halves:
-            nc.vector.tensor_tensor(
-                out=result[:, cols], in0=chorus[last][:, cols], in1=verse[last][:, cols], op=ALU.subtract
-            )
-        nc.sync.dma_start(out=out[P * last : P * (last + 1), :], in_=result[:])
+            for cols in col_halves:
+                larger(i, cols)
+            if i < M_TILES - 2:
+                weigh_on_gpsimd(i)
+                finish_on_tensor(i)
+            elif i < M_TILES - 1:
+                finish_on_gpsimd(i)
+            else:
+                finish_on_vector(i)

@@ -24,6 +24,7 @@ HALVES = S // BANK
 M_TILES = S2 // P
 TAB_S_FIRST = (48, 64, 80)
 EARLY = 256
+TURNED = 256
 W1_PIECES = [[(0, H)], [(0, H)], [(0, H // 2), (H // 2, H)]]
 
 
@@ -76,8 +77,8 @@ def tile_list_karaoke_style_scores_kernel(
             rows = w1[512 * a : 512 * (a + 1), c0:c1]
             nc.sync.dma_start(out=w1_raw[a][piece][:], in_=rows.rearrange("(p j) c -> p j c", j=4))
 
-        def place_rows(plane, gathered, first, q):
-            nc.sync.dma_start(
+        def place_rows(queue, plane, gathered, first, q):
+            queue.dma_start(
                 out=plane[32 * q : 32 * q + 4, :].bitcast(I32),
                 in_=gathered[first + 4 * q : first + 4 * q + 4, :].bitcast(I32),
             )
@@ -105,19 +106,21 @@ def tile_list_karaoke_style_scores_kernel(
         v2_s_rows = keep.tile([P, S2], U8, name="v2_s_rows", align_bytes=64)
         nc.vector.tensor_copy(v2_s_rows[:], tab2_s[:].indirect(idx2[:]))
 
-        moves = [(a, q) for a in range(PASSES) for q in range(4)]
+        moves = [(a, q) for a in range(PASSES - 1) for q in range(4)]
         for a, q in moves[:6]:
-            place_rows(v_planes[:, a, :], v_s, TAB_S_FIRST[a], q)
+            place_rows(nc.sync, v_planes[:, a, :], v_s, TAB_S_FIRST[a], q)
         load_tab(2)
         for a, q in moves[6:]:
-            place_rows(v_planes[:, a, :], v_s, TAB_S_FIRST[a], q)
+            place_rows(nc.sync, v_planes[:, a, :], v_s, TAB_S_FIRST[a], q)
+        for q in range(4):
+            place_rows(nc.gpsimd, v_planes[:, PASSES - 1, :], v_s, TAB_S_FIRST[PASSES - 1], q)
         load_w1(0, 0)
         load_w1(1, 0)
         load_w1(2, 0)
         load_w1(2, 1)
         nc.sync.dma_start(out=tab2_w[:], in_=tab2_words[0].rearrange("p t i -> p (t i)").bitcast(I32))
         for q in range(4):
-            place_rows(v2_s[:], v2_s_rows, 112, q)
+            place_rows(nc.sync, v2_s[:], v2_s_rows, 112, q)
         nc.sync.dma_start(p2[:], pos2)
         for g in range(2):
             rows = song[g * S2 // 2 : (g + 1) * S2 // 2, :]
@@ -238,7 +241,7 @@ def tile_list_karaoke_style_scores_kernel(
                 return v2_early[:, P * i : P * (i + 1)]
             return v2_late[:, P * i - EARLY : P * (i + 1) - EARLY]
 
-        e, verse, chorus = {}, {}, {}
+        e, verse, chorus, result = {}, {}, {}, {}
         col_halves = [slice(0, NP // 2), slice(NP // 2, NP)]
 
         def scores(i):
@@ -269,59 +272,56 @@ def tile_list_karaoke_style_scores_kernel(
         def larger(i, cols):
             nc.vector.tensor_tensor(out=chorus[i][:, cols], in0=chorus[i][:, cols], in1=verse[i][:, cols], op=ALU.max)
 
-        def weigh_on_gpsimd(i):
-            nc.gpsimd.tensor_tensor(out=chorus[i][:], in0=chorus[i][:], in1=song_rows(i), op=ALU.mult)
-            nc.gpsimd.tensor_scalar(
-                out=verse[i][:], in0=verse[i][:], scalar1=-1.0, scalar2=0.0, op0=ALU.mult, op1=ALU.add
+        def weigh(engine, i, cols):
+            engine.tensor_tensor(
+                out=chorus[i][:, cols], in0=chorus[i][:, cols], in1=song_rows(i)[:, cols], op=ALU.mult
             )
 
-        def finish_on_tensor(i):
+        def subtract_on_vector(i, cols):
+            nc.vector.tensor_tensor(
+                out=result[i][:, cols], in0=chorus[i][:, cols], in1=verse[i][:, cols], op=ALU.subtract
+            )
+
+        def subtract_on_tensor(i):
+            blocks = [slice(c, c + P) for c in range(0, TURNED, P)]
+            negated = ring.tile([P, TURNED], F32, name="negated")
+            nc.scalar.activation(out=negated[:], in_=verse[i][:, 0:TURNED], func=ACT.Copy, scale=-1.0)
             turned = bank_tile(4 + i % 2, f"turned{i}")
-            for k, term in enumerate((chorus[i], verse[i])):
-                for c in range(4):
+            for k, term in enumerate((negated, chorus[i])):
+                for block in blocks:
                     nc.tensor.matmul(
-                        turned[:, P * c : P * (c + 1)], lhsT=term[:, P * c : P * (c + 1)], rhs=ident[:],
-                        is_transpose=True, start=(k == 0 and c == 0), stop=(k == 1 and c == 3),
+                        turned[:, block], lhsT=term[:, block], rhs=ident[:], is_transpose=True,
+                        start=(k == 0 and block == blocks[0]), stop=(k == 1 and block == blocks[-1]),
                     )
-            turned_sb = ring.tile([P, NP], F32, name="turned_sb")
-            nc.scalar.copy(out=turned_sb[:], in_=turned[:])
+            turned_sb = ring.tile([P, TURNED], F32, name="turned_sb")
+            nc.scalar.copy(out=turned_sb[:], in_=turned[:, 0:TURNED])
             upright = bank_tile(6 + i % 2, f"upright{i}")
-            for c in range(4):
-                nc.tensor.transpose(upright[:, P * c : P * (c + 1)], turned_sb[:, P * c : P * (c + 1)], ident[:])
-            result = ring.tile([P, NP], F32, name="result")
-            nc.scalar.copy(out=result[:], in_=upright[:])
-            nc.sync.dma_start(out=out[P * i : P * (i + 1), :], in_=result[:])
+            for block in blocks:
+                nc.tensor.transpose(upright[:, block], turned_sb[:, block], ident[:])
+            nc.scalar.copy(out=result[i][:, 0:TURNED], in_=upright[:, 0:TURNED])
 
-        def finish_on_gpsimd(i):
-            result = ring.tile([P, NP], F32, name="result")
-            nc.gpsimd.tensor_tensor(out=chorus[i][:], in0=chorus[i][:], in1=song_rows(i), op=ALU.mult)
-            nc.gpsimd.tensor_tensor(out=result[:], in0=chorus[i][:], in1=verse[i][:], op=ALU.subtract)
-            nc.sync.dma_start(out=out[P * i : P * (i + 1), :], in_=result[:])
+        def store(i):
+            nc.sync.dma_start(out=out[P * i : P * (i + 1), :], in_=result[i][:])
 
-        def finish_on_vector(i):
-            result = ring.tile([P, NP], F32, name="result")
-            for cols in col_halves:
-                nc.vector.tensor_tensor(
-                    out=chorus[i][:, cols], in0=chorus[i][:, cols], in1=song_rows(i)[:, cols], op=ALU.mult
-                )
-            for cols in col_halves:
-                nc.vector.tensor_tensor(
-                    out=result[:, cols], in0=chorus[i][:, cols], in1=verse[i][:, cols], op=ALU.subtract
-                )
-            nc.sync.dma_start(out=out[P * i : P * (i + 1), :], in_=result[:])
-
+        last = M_TILES - 1
         scores(0)
         scores(1)
         for i in range(M_TILES):
             if i + 2 < M_TILES:
                 scores(i + 2)
             pick(i)
+            if i > 0:
+                subtract_on_vector(i - 1, slice(TURNED if i < last else 0, NP))
+                store(i - 1)
             for cols in col_halves:
                 larger(i, cols)
-            if i < M_TILES - 2:
-                weigh_on_gpsimd(i)
-                finish_on_tensor(i)
-            elif i < M_TILES - 1:
-                finish_on_gpsimd(i)
-            else:
-                finish_on_vector(i)
+            result[i] = ring.tile([P, NP], F32, name="result")
+            if i < last:
+                weigh(nc.gpsimd, i, slice(0, NP))
+            if i < last - 1:
+                subtract_on_tensor(i)
+        for cols in col_halves:
+            weigh(nc.vector, last, cols)
+        for cols in col_halves:
+            subtract_on_vector(last, cols)
+        store(last)

@@ -24,7 +24,7 @@ HALVES = S // BANK
 M_TILES = S2 // P
 TAB_S_FIRST = (48, 64, 80)
 EARLY = 256
-TURNED = 256
+TURNED = 384
 W1_PIECES = [[(0, H)], [(0, H)], [(0, H // 2), (H // 2, H)]]
 
 
@@ -150,8 +150,8 @@ def tile_list_karaoke_style_scores_kernel(
         def round_w1(copy, a, piece):
             c0, c1 = W1_PIECES[a][piece]
             copy(
-                out=w1_bf[a][:].rearrange("p (t m j) -> p m j t", t=4, j=4)[:, c0 // 4 : c1 // 4],
-                in_=w1_raw[a][piece][:].rearrange("p j (m t) -> p m j t", t=4),
+                out=w1_bf[a][:].rearrange("p (t m j) -> p m t j", t=4, j=4)[:, c0 // 4 : c1 // 4],
+                in_=w1_raw[a][piece][:].rearrange("p j (m t) -> p m t j", t=4),
             )
 
         def quantise_w1(a):
@@ -207,8 +207,8 @@ def tile_list_karaoke_style_scores_kernel(
                 for t in range(4):
                     s_pass(a, u, t)
 
-        h_rows = [keep.tile([P, 4, BANK], BF16, name=f"h_rows{u}", tag=f"h_rows{u}", align_bytes=64) for u in range(HALVES)]
-        h_bf = [keep.tile([P, BANK, 4], BF16, name=f"h_bf{u}", align_bytes=64) for u in range(HALVES)]
+        h_rows = [keep.tile([P, 4, BANK], BF16, name=f"h_rows{u}", align_bytes=64) for u in range(HALVES)]
+        h_bf = [keep.tile([P, BANK, 4], BF16, name=f"h_bf{u}", tag=f"h_bf{u}", align_bytes=64) for u in range(HALVES)]
         h_w = [keep.tile([P, BANK], U32, name=f"h_w{u}", align_bytes=64) for u in range(HALVES)]
         h_s = [keep.tile([P, BANK], U8, name=f"h_s{u}", align_bytes=64) for u in range(HALVES)]
 
@@ -226,14 +226,18 @@ def tile_list_karaoke_style_scores_kernel(
                 )
         v2_early = keep.tile([P, EARLY], U32, name="v2_early", align_bytes=64)
         nc.vector.tensor_copy(v2_early[:], tab2_w[:].bitcast(U32).indirect(idx2[:, 0 : EARLY // 16]))
-        weave(nc.scalar.copy, 0, 0, BANK)
-        weave(nc.vector.tensor_copy, 1, 0, 384)
-        weave(nc.scalar.copy, 1, 384, BANK)
-        for u in range(HALVES):
+
+        def quantise_h(u):
             nc.vector.quantize_mx(
                 out=h_w[u][:].bitcast(FP8X4), scales=h_s[u][:], in_=h_bf[u][:].rearrange("p c t -> p (c t)")
             )
-        v2_late = keep.tile([P, S2 - EARLY], U32, name="v2_late", tag="h_rows1", align_bytes=64)
+
+        weave(nc.scalar.copy, 0, 0, BANK)
+        quantise_h(0)
+        weave(nc.vector.tensor_copy, 1, 0, 320)
+        weave(nc.scalar.copy, 1, 320, BANK)
+        quantise_h(1)
+        v2_late = keep.tile([P, S2 - EARLY], U32, name="v2_late", tag="h_bf1", align_bytes=64)
         nc.vector.tensor_copy(v2_late[:], tab2_w[:].bitcast(U32).indirect(idx2[:, EARLY // 16 :]))
 
         def v2_words(i):
@@ -300,8 +304,8 @@ def tile_list_karaoke_style_scores_kernel(
                 nc.tensor.transpose(upright[:, block], turned_sb[:, block], ident[:])
             nc.scalar.copy(out=result[i][:, 0:TURNED], in_=upright[:, 0:TURNED])
 
-        def store(i):
-            nc.sync.dma_start(out=out[P * i : P * (i + 1), :], in_=result[i][:])
+        def store(i, cols):
+            nc.sync.dma_start(out=out[P * i : P * (i + 1), cols], in_=result[i][:, cols])
 
         last = M_TILES - 1
         scores(0)
@@ -312,7 +316,7 @@ def tile_list_karaoke_style_scores_kernel(
             pick(i)
             if i > 0:
                 subtract_on_vector(i - 1, slice(TURNED if i < last else 0, NP))
-                store(i - 1)
+                store(i - 1, slice(0, NP))
             for cols in col_halves:
                 larger(i, cols)
             result[i] = ring.tile([P, NP], F32, name="result")
@@ -324,4 +328,4 @@ def tile_list_karaoke_style_scores_kernel(
             weigh(nc.vector, last, cols)
         for cols in col_halves:
             subtract_on_vector(last, cols)
-        store(last)
+            store(last, cols)

from contextlib import ExitStack

import concourse.mybir as mybir
from concourse.masks import make_identity

K, T, H, S, S2, T3, NP = 1536, 4096, 512, 1024, 1024, 2048, 512
FLOPS = 2 * (2 * K * H * S + H * S2 * S)

F32 = mybir.dt.float32
BF16 = mybir.dt.bfloat16
I32 = mybir.dt.int32
U32 = mybir.dt.uint32
U16 = mybir.dt.uint16
U8 = mybir.dt.uint8
FP8X4 = mybir.dt.float8_e4m3fn_x4
FP4X4 = mybir.dt.float4_e2m1fn_x4
ALU = mybir.AluOpType
ACT = mybir.ActivationFunctionType

P = 128
PASSES = K // 512
BANK = 512
HALVES = S // BANK
M_TILES = S2 // P
TAB_S_FIRST = (48, 64, 80)
EARLY = 256
TURNED = 384
W1_PIECES = [[(0, H)], [(0, H)], [(0, H // 2), (H // 2, H)]]


def tile_list_karaoke_style_scores_kernel(
    tc, tab_words, tab_scales, offs, tab2_words, tab2_scales, offs2, pos1, pos2, w1, w4_words, w4_scales, bias, gain, song, out
):
    nc = tc.nc
    with ExitStack() as ctx:
        keep = ctx.enter_context(tc.tile_pool(name="keep", bufs=1))
        ring = ctx.enter_context(tc.tile_pool(name="ring", bufs=4))
        psum = ctx.enter_context(tc.psum_pool(name="psum", bufs=1))

        def bank_tile(index, name):
            return psum.tile([P, BANK], F32, name=name, tag=f"bank{index}")

        idx = keep.tile([P, S // 16], U16, name="idx")
        idx2 = keep.tile([P, S2 // 16], U16, name="idx2")
        p1 = keep.tile([P, NP // 16], U16, name="p1")
        p2 = keep.tile([P, NP // 16], U16, name="p2")
        tab_w = [keep.tile([P, T], I32, name=f"tab_w{a}", align_bytes=64) for a in range(PASSES)]
        tab_s = keep.tile([P, T], U8, name="tab_s", align_bytes=64)
        tab2_w = keep.tile([P, T3], I32, name="tab2_w", align_bytes=64)
        tab2_s = keep.tile([P, T3], U8, name="tab2_s", tag="v_w2_0", align_bytes=64)
        w4_raw = keep.tile([P, PASSES, 2 * H], U8, name="w4_raw", align_bytes=64)
        w4_s_raw = keep.tile([P, PASSES, H], U8, name="w4_s_raw", tag="v_w1_0", align_bytes=64)
        w1_raw = [
            [keep.tile([P, 4, c1 - c0], F32, name=f"w1_raw{a}_{c0}") for c0, c1 in W1_PIECES[a]] for a in range(PASSES)
        ]
        bias_t = keep.tile([P, 4], F32, name="bias_t")
        gain_t = keep.tile([P, 4], F32, name="gain_t")
        song_t = [keep.tile([P, M_TILES // 2, NP], F32, name=f"song_t{g}") for g in range(2)]
        v_planes = keep.tile([P, PASSES, S], U8, name="v_planes", align_bytes=64)
        ident = keep.tile([P, P], F32, name="ident")

        v2_s = keep.tile([P, S2], U8, name="v2_s", align_bytes=64)

        nc.vector.memset(w4_s_raw[:].rearrange("p a c -> p (a c)").bitcast(I32), 0)
        nc.vector.memset(tab_s[0:48, :].bitcast(I32), 0)
        nc.gpsimd.memset(tab_s[96:P, :].bitcast(I32), 0)
        nc.gpsimd.memset(tab2_s[0:112, :].bitcast(I32), 0)
        nc.gpsimd.memset(v_planes[:].rearrange("p a c -> p (a c)").bitcast(I32), 0)
        nc.gpsimd.memset(v2_s[:].bitcast(I32), 0)
        make_identity(nc, ident[:])

        def load_tab(a):
            nc.sync.dma_start(out=tab_w[a][:], in_=tab_words[a].rearrange("p t i -> p (t i)").bitcast(I32))

        def load_w1(a, piece):
            c0, c1 = W1_PIECES[a][piece]
            rows = w1[512 * a : 512 * (a + 1), c0:c1]
            nc.sync.dma_start(out=w1_raw[a][piece][:], in_=rows.rearrange("(p j) c -> p j c", j=4))

        def place_rows(queue, plane, gathered, first, q):
            queue.dma_start(
                out=plane[32 * q : 32 * q + 4, :].bitcast(I32),
                in_=gathered[first + 4 * q : first + 4 * q + 4, :].bitcast(I32),
            )

        scale_rows = tab_scales.rearrange("a q t -> (a q) t").bitcast(I32)
        nc.sync.dma_start(idx[:], offs)
        nc.sync.dma_start(out=tab_s[48:64, :].bitcast(I32), in_=scale_rows[0:16, :])
        nc.sync.dma_start(out=tab_s[64:96, :].bitcast(I32), in_=scale_rows[16:48, :])
        nc.sync.dma_start(idx2[:], offs2)
        nc.sync.dma_start(out=tab2_s[112:P, :].bitcast(I32), in_=tab2_scales[0].bitcast(I32))
        nc.sync.dma_start(out=w4_raw[:].bitcast(I32), in_=w4_words.rearrange("a p c -> p a c").bitcast(I32))
        nc.sync.dma_start(out=bias_t[:], in_=bias.rearrange("(p t) -> p t", t=4))
        load_tab(0)
        for q in range(4):
            nc.sync.dma_start(
                out=w4_s_raw[32 * q : 32 * q + 4, :, :].bitcast(I32),
                in_=w4_scales[:, 4 * q : 4 * q + 4, :].rearrange("a r c -> r a c").bitcast(I32),
            )
        nc.sync.dma_start(out=gain_t[:], in_=gain.rearrange("(p t) -> p t", t=4))
        nc.sync.dma_start(p1[:], pos1)
        load_tab(1)

        v_s = keep.tile([P, S], U8, name="v_s", align_bytes=64)
        nc.vector.tensor_copy(v_s[:], tab_s[:].indirect(idx[:]))
        v2_s_rows = keep.tile([P, S2], U8, name="v2_s_rows", align_bytes=64)
        nc.vector.tensor_copy(v2_s_rows[:], tab2_s[:].indirect(idx2[:]))

        moves = [(a, q) for a in range(PASSES - 1) for q in range(4)]
        for a, q in moves[:6]:
            place_rows(nc.sync, v_planes[:, a, :], v_s, TAB_S_FIRST[a], q)
        load_tab(2)
        for a, q in moves[6:]:
            place_rows(nc.sync, v_planes[:, a, :], v_s, TAB_S_FIRST[a], q)
        for q in range(4):
            place_rows(nc.gpsimd, v_planes[:, PASSES - 1, :], v_s, TAB_S_FIRST[PASSES - 1], q)
        load_w1(0, 0)
        load_w1(1, 0)
        load_w1(2, 0)
        load_w1(2, 1)
        nc.sync.dma_start(out=tab2_w[:], in_=tab2_words[0].rearrange("p t i -> p (t i)").bitcast(I32))
        for q in range(4):
            place_rows(nc.sync, v2_s[:], v2_s_rows, 112, q)
        nc.sync.dma_start(p2[:], pos2)
        for g in range(2):
            rows = song[g * S2 // 2 : (g + 1) * S2 // 2, :]
            nc.sync.dma_start(out=song_t[g][:], in_=rows.rearrange("(c p) n -> p c n", p=P))

        w4_w = keep.tile([P, PASSES, 2 * H], U8, name="w4_w", align_bytes=64)
        w4_s = keep.tile([P, PASSES, H], U8, name="w4_s", align_bytes=64)
        nc.vector.tensor_copy(
            out=w4_w[:].bitcast(U16).rearrange("p a (t m) -> p t a m", t=4),
            in_=w4_raw[:].bitcast(U16).rearrange("p a (m t) -> p t a m", t=4),
        )
        nc.vector.tensor_copy(
            out=w4_s[:].rearrange("p a (t m) -> p t a m", t=4),
            in_=w4_s_raw[:].rearrange("p a (m t) -> p t a m", t=4),
        )

        v_w = [[] for a in range(PASSES)]
        w1_bf = [keep.tile([P, 4 * H], BF16, name=f"w1_bf{a}", align_bytes=64) for a in range(PASSES)]
        w1_w = [keep.tile([P, H], U32, name=f"w1_w{a}", align_bytes=64) for a in range(PASSES)]
        w1_s = [keep.tile([P, H], U8, name=f"w1_s{a}", align_bytes=64) for a in range(PASSES)]

        def gather_tab(a):
            for u in range(HALVES):
                v_w[a].append(keep.tile([P, BANK], U32, name=f"v_w{a}_{u}", tag=f"v_w{a}_{u}", align_bytes=64))
                nc.vector.tensor_copy(v_w[a][u][:], tab_w[a][:].bitcast(U32).indirect(idx[:, 32 * u : 32 * (u + 1)]))

        def round_w1(copy, a, piece):
            c0, c1 = W1_PIECES[a][piece]
            copy(
                out=w1_bf[a][:].rearrange("p (t m j) -> p m t j", t=4, j=4)[:, c0 // 4 : c1 // 4],
                in_=w1_raw[a][piece][:].rearrange("p j (m t) -> p m t j", t=4),
            )

        def quantise_w1(a):
            nc.vector.quantize_mx(out=w1_w[a][:].bitcast(FP8X4), scales=w1_s[a][:], in_=w1_bf[a][:])

        b_acc = [[bank_tile(4 * u + t, f"b_acc{u}_{t}") for t in range(4)] for u in range(HALVES)]

        def b_pass(a):
            for u in range(HALVES):
                for t in range(4):
                    nc.tensor.matmul_mx(
                        out=b_acc[u][t][:],
                        lhsT=w4_w[:, a, 2 * P * t : 2 * P * (t + 1)].bitcast(FP4X4),
                        lhsT_scale=w4_s[:, a, P * t : P * (t + 1)],
                        rhs=v_w[a][u][:].bitcast(FP8X4),
                        rhs_scale=v_planes[:, a, BANK * u : BANK * (u + 1)],
                        start=(a == 0),
                        stop=(a == PASSES - 1),
                    )

        gather_tab(0)
        b_pass(0)
        gather_tab(1)
        b_pass(1)
        gather_tab(2)
        b_pass(2)

        th = [[keep.tile([P, BANK], F32, name=f"th{u}_{t}") for t in range(4)] for u in range(HALVES)]
        for u in range(HALVES):
            for t in range(4):
                nc.scalar.activation(out=th[u][t][:], in_=b_acc[u][t][:], func=ACT.Tanh, bias=bias_t[:, t : t + 1])

        for a in range(PASSES):
            for piece in range(len(W1_PIECES[a])):
                round_w1(nc.scalar.copy if (a, piece) == (2, 0) else nc.vector.tensor_copy, a, piece)
            quantise_w1(a)

        s_acc = [[bank_tile(4 * u + t, f"s_acc{u}_{t}") for t in range(4)] for u in range(HALVES)]

        def s_pass(a, u, t):
            nc.tensor.matmul_mx(
                out=s_acc[u][t][:],
                lhsT=w1_w[a][:, P * t : P * (t + 1)].bitcast(FP8X4),
                lhsT_scale=w1_s[a][:, P * t : P * (t + 1)],
                rhs=v_w[a][u][:].bitcast(FP8X4),
                rhs_scale=v_planes[:, a, BANK * u : BANK * (u + 1)],
                start=(a == 0),
                stop=(a == PASSES - 1),
            )

        for a in range(PASSES):
            for u in range(HALVES):
                for t in range(4):
                    s_pass(a, u, t)

        h_rows = [keep.tile([P, 4, BANK], BF16, name=f"h_rows{u}", align_bytes=64) for u in range(HALVES)]
        h_bf = [keep.tile([P, BANK, 4], BF16, name=f"h_bf{u}", tag=f"h_bf{u}", align_bytes=64) for u in range(HALVES)]
        h_w = [keep.tile([P, BANK], U32, name=f"h_w{u}", align_bytes=64) for u in range(HALVES)]
        h_s = [keep.tile([P, BANK], U8, name=f"h_s{u}", align_bytes=64) for u in range(HALVES)]

        def weave(copy, u, c0, c1):
            copy(
                out=h_bf[u][:, c0:c1, :].rearrange("p (c i) t -> p c t i", i=4),
                in_=h_rows[u][:, :, c0:c1].rearrange("p t (c i) -> p c t i", i=4),
            )

        for u in range(HALVES):
            for t in range(4):
                nc.vector.scalar_tensor_tensor(
                    out=h_rows[u][:, t, :], in0=th[u][t][:], scalar=gain_t[:, t : t + 1], in1=s_acc[u][t][:],
                    op0=ALU.mult, op1=ALU.add,
                )
        v2_early = keep.tile([P, EARLY], U32, name="v2_early", align_bytes=64)
        nc.vector.tensor_copy(v2_early[:], tab2_w[:].bitcast(U32).indirect(idx2[:, 0 : EARLY // 16]))

        def quantise_h(u):
            nc.vector.quantize_mx(
                out=h_w[u][:].bitcast(FP8X4), scales=h_s[u][:], in_=h_bf[u][:].rearrange("p c t -> p (c t)")
            )

        weave(nc.scalar.copy, 0, 0, BANK)
        quantise_h(0)
        weave(nc.vector.tensor_copy, 1, 0, 320)
        weave(nc.scalar.copy, 1, 320, BANK)
        quantise_h(1)
        v2_late = keep.tile([P, S2 - EARLY], U32, name="v2_late", tag="h_bf1", align_bytes=64)
        nc.vector.tensor_copy(v2_late[:], tab2_w[:].bitcast(U32).indirect(idx2[:, EARLY // 16 :]))

        def v2_words(i):
            if P * i < EARLY:
                return v2_early[:, P * i : P * (i + 1)]
            return v2_late[:, P * i - EARLY : P * (i + 1) - EARLY]

        e, verse, chorus, result = {}, {}, {}, {}
        col_halves = [slice(0, NP // 2), slice(NP // 2, NP)]

        def scores(i):
            e[i] = ring.tile([P, S], F32, name="e")
            for u in range(HALVES):
                e_acc = bank_tile((HALVES * i + u) % 4, f"e_acc{i}_{u}")
                nc.tensor.matmul_mx(
                    out=e_acc[:],
                    lhsT=v2_words(i).bitcast(FP8X4),
                    lhsT_scale=v2_s[:, P * i : P * (i + 1)],
                    rhs=h_w[u][:].bitcast(FP8X4),
                    rhs_scale=h_s[u][:],
                    start=True,
                    stop=True,
                )
                nc.scalar.copy(out=e[i][:, BANK * u : BANK * (u + 1)], in_=e_acc[:])

        def pick(i):
            verse[i] = ring.tile([P, NP], F32, name="verse")
            chorus[i] = ring.tile([P, NP], F32, name="chorus")
            nc.vector.tensor_copy(verse[i][:], e[i][:].indirect(p1[:]))
            for g, cols in enumerate(col_halves):
                nc.vector.tensor_copy(chorus[i][:, cols], e[i][:].indirect(p2[:, 16 * g : 16 * (g + 1)]))

        def song_rows(i):
            return song_t[i // 4][:, i % 4, :]

        def larger(i, cols):
            nc.vector.tensor_tensor(out=chorus[i][:, cols], in0=chorus[i][:, cols], in1=verse[i][:, cols], op=ALU.max)

        def weigh(engine, i, cols):
            engine.tensor_tensor(
                out=chorus[i][:, cols], in0=chorus[i][:, cols], in1=song_rows(i)[:, cols], op=ALU.mult
            )

        def subtract_on_vector(i, cols):
            nc.vector.tensor_tensor(
                out=result[i][:, cols], in0=chorus[i][:, cols], in1=verse[i][:, cols], op=ALU.subtract
            )

        def subtract_on_tensor(i):
            blocks = [slice(c, c + P) for c in range(0, TURNED, P)]
            negated = ring.tile([P, TURNED], F32, name="negated")
            nc.scalar.activation(out=negated[:], in_=verse[i][:, 0:TURNED], func=ACT.Copy, scale=-1.0)
            turned = bank_tile(4 + i % 2, f"turned{i}")
            for k, term in enumerate((negated, chorus[i])):
                for block in blocks:
                    nc.tensor.matmul(
                        turned[:, block], lhsT=term[:, block], rhs=ident[:], is_transpose=True,
                        start=(k == 0 and block == blocks[0]), stop=(k == 1 and block == blocks[-1]),
                    )
            turned_sb = ring.tile([P, TURNED], F32, name="turned_sb")
            nc.scalar.copy(out=turned_sb[:], in_=turned[:, 0:TURNED])
            upright = bank_tile(6 + i % 2, f"upright{i}")
            for block in blocks:
                nc.tensor.transpose(upright[:, block], turned_sb[:, block], ident[:])
            nc.scalar.copy(out=result[i][:, 0:TURNED], in_=upright[:, 0:TURNED])

        def store(i, cols):
            nc.sync.dma_start(out=out[P * i : P * (i + 1), cols], in_=result[i][:, cols])

        last = M_TILES - 1
        scores(0)
        scores(1)
        for i in range(M_TILES):
            if i + 2 < M_TILES:
                scores(i + 2)
            pick(i)
            if i > 0:
                subtract_on_vector(i - 1, slice(TURNED if i < last else 0, NP))
                store(i - 1, slice(0, NP))
            for cols in col_halves:
                larger(i, cols)
            result[i] = ring.tile([P, NP], F32, name="result")
            if i < last:
                weigh(nc.gpsimd, i, slice(0, NP))
            if i < last - 1:
                subtract_on_tensor(i)
        for cols in col_halves:
            weigh(nc.vector, last, cols)
        for cols in col_halves:
            subtract_on_vector(last, cols)
            store(last, cols)
